import numpy as np
import ml_dtypes


def mxq(x, axis, fmt="e4m3"):
    dtype, down = {"e4m3": (ml_dtypes.float8_e4m3fn, 7), "e5m2": (ml_dtypes.float8_e5m2, 14)}[fmt]
    v = np.moveaxis(np.asarray(x, np.float32).astype(ml_dtypes.bfloat16).astype(np.float64), axis, -1)
    blocks = v.reshape(v.shape[:-1] + (-1, 32))
    amax = np.abs(blocks).max(-1, keepdims=True)
    byte = np.maximum(np.where(amax > 0, np.frexp(amax)[1] - 1 + 127, 0) - down, 1)
    scale = np.exp2(byte - 127.0)
    codes = (blocks / scale).astype(np.float32).astype(dtype).astype(np.float64)
    return np.moveaxis((codes * scale).reshape(v.shape), -1, axis)


WIDE = False


def mx_kscale(k):
    if not WIDE:
        return np.ones(k)
    levels = np.array([30, -30])
    if k % 512:
        return np.exp2(np.random.permutation(np.resize(levels, k // 32))).repeat(32)
    a = np.empty((k // 512, 16))
    for p in range(k // 512):
        a[p, :8] = np.random.permutation(np.resize(levels, 8))
        for g in range(8):
            far = levels[np.abs(levels - a[p, g]) >= 10]
            a[p, g + 8] = far[np.random.randint(len(far))]
    return np.exp2(a.ravel()).repeat(32)


def f64(x):
    return np.asarray(x).astype(np.float64)


def striped(idx):
    return np.tile(np.asarray(idx).reshape(-1, 16).T, (8, 1)).astype(np.uint16)


def unstriped(offs):
    return offs[:16].T.reshape(-1).astype(np.int64)


E2M1 = np.array([0.0, 0.5, 1.0, 1.5, 2.0, 3.0, 4.0, 6.0, -0.0, -0.5, -1.0, -1.5, -2.0, -3.0, -4.0, -6.0])


def pack_weight(w, fmt):
    k, n = w.shape
    w = f64(np.asarray(w, np.float32).astype(ml_dtypes.bfloat16)).reshape(k // 32, 32, n)
    amax = np.abs(w).max(1)
    if fmt in ("e4m3", "e5m2"):
        byte = np.frexp(amax)[1] - 1 + 127 - (7 if fmt == "e4m3" else 14)
    else:
        mant, ex = np.frexp(amax / 6.0)
        byte = np.where(mant > 0.5, ex, ex - 1) + 127
    byte = np.clip(np.where(amax > 0, byte, 1), 1, 254)
    scaled = (w * np.exp2(127.0 - byte)[:, None, :]).reshape(k, n).astype(np.float32)
    by_word = np.ascontiguousarray(scaled.reshape(k // 512, 128, 4, n).transpose(0, 1, 3, 2))
    if fmt in ("e4m3", "e5m2"):
        words = by_word.astype(ml_dtypes.float8_e4m3fn if fmt == "e4m3" else ml_dtypes.float8_e5m2).view(np.uint8)
    else:
        c = by_word.astype(ml_dtypes.float4_e2m1fn).view(np.uint8) & 0xF
        words = (c[..., 0::2] | (c[..., 1::2] << 4)).reshape(k // 512, 128, 2 * n)
    return np.ascontiguousarray(words), np.ascontiguousarray(byte.astype(np.uint8).reshape(k // 512, 16, n))


def unpack_weight(words, scales, fmt):
    g, _, n = scales.shape
    words = np.ascontiguousarray(words).reshape(g, 128, n, -1)
    if fmt in ("e4m3", "e5m2"):
        vals = words.view(ml_dtypes.float8_e4m3fn if fmt == "e4m3" else ml_dtypes.float8_e5m2).astype(np.float64)
    else:
        nib = np.empty((g, 128, n, 4), np.uint8)
        nib[..., 0::2] = words & 0xF
        nib[..., 1::2] = words >> 4
        vals = E2M1[nib]
    vals = vals * np.repeat(np.exp2(scales.astype(np.float64) - 127.0), 8, axis=1)[..., None]
    return vals.transpose(0, 1, 3, 2).reshape(g * 512, n)


K, T, J, N, C = 1024, 1024, 256, 256, 512


def setup_inputs():
    n = np.random.standard_normal
    idx = np.random.permutation(T)[:J]
    idx2 = np.random.permutation(C)[:N]
    fk = mx_kscale(K)
    xtp = pack_weight(n((K, T)) * np.random.uniform(0.4, 1.6, (1, T)) / fk[:, None], "e4m3")
    wap = pack_weight(n((K, N)) * 1 / np.sqrt(K) * fk[:, None], "e5m2")
    return {
        "xt_words": xtp[0],
        "xt_scales": xtp[1],
        "wa_words": wap[0],
        "wa_scales": wap[1],
        "wb": (n((K, N)) * 1 / np.sqrt(K) * fk[:, None]).astype(np.float32),
        "bi": (np.random.uniform(-0.6, 0.6, (1, N))).astype(np.float32),
        "tb": (1.0 * n((J, C))).astype(np.float32),
        "offs": striped(idx),
        "offs2": striped(idx2),
    }


def reference(xt_words, xt_scales, wa_words, wa_scales, wb, bi, tb, offs, offs2):
    idx = unstriped(offs)
    idx2 = unstriped(offs2)
    xtu = unpack_weight(xt_words, xt_scales, "e4m3")
    wau = unpack_weight(wa_words, wa_scales, "e5m2")
    xtidxg = xtu[:, idx]
    a = xtidxg.T @ wau
    wbq = mxq(f64(wb), 0, "e5m2")
    b0 = xtidxg.T @ wbq
    b2 = b0 + f64(bi)
    y = (a + 0.5 * b2) * f64(tb)[:, idx2]
    return y

@@ -1,0 +1,158 @@
+from contextlib import ExitStack
+
+import concourse.mybir as mybir
+from concourse.masks import make_identity
+
+K, T, J, N, C = 1024, 1024, 256, 256, 512
+FLOPS = 2 * 2 * K * J * N
+
+F32 = mybir.dt.float32
+BF16 = mybir.dt.bfloat16
+I32 = mybir.dt.int32
+U32 = mybir.dt.uint32
+U16 = mybir.dt.uint16
+U8 = mybir.dt.uint8
+E4M3 = mybir.dt.float8_e4m3fn_x4
+E5M2 = mybir.dt.float8_e5m2_x4
+ADD = mybir.AluOpType.add
+MULT = mybir.AluOpType.mult
+COPY = mybir.ActivationFunctionType.Copy
+
+P = 128
+PACK = 4
+K_PASS = P * PACK
+PASSES = K // K_PASS
+J_TILES = J // P
+LIST_COLS = J // 16
+QUADRANTS = 4
+
+
+def tile_list_rows_onetoken_tablegate_kernel(
+    tc, xt_words, xt_scales, wa_words, wa_scales, wb, bi, tb, offs, offs2, out
+):
+    nc = tc.nc
+    with ExitStack() as ctx:
+        lists = ctx.enter_context(tc.tile_pool(name="lists", bufs=1))
+        sb = ctx.enter_context(tc.tile_pool(name="sb", bufs=1))
+        ps = ctx.enter_context(tc.psum_pool(name="ps", bufs=1))
+
+        tokens = lists.tile([P, LIST_COLS], U16, name="tokens")
+        entries = lists.tile([P, N // 16], U16, name="entries")
+
+        xt_plane = sb.tile([P, PASSES, T], U8, name="xt_plane", align_bytes=64)
+        wa_plane = sb.tile([P, PASSES, N], U8, name="wa_plane", align_bytes=64)
+        nc.vector.memset(xt_plane[:].rearrange("p z c -> p (z c)").bitcast(I32), 0)
+        nc.vector.memset(wa_plane[:].rearrange("p z c -> p (z c)").bitcast(I32), 0)
+
+        nc.sync.dma_start(tokens[:], offs)
+        xt_rows = xt_scales.bitcast(I32)
+        for q in range(QUADRANTS):
+            nc.scalar.dma_start(
+                xt_plane[32 * q : 32 * q + 4, :, :].bitcast(I32),
+                xt_rows[:, 4 * q : 4 * q + 4, :].rearrange("z r c -> r z c"),
+            )
+        wa_rows = wa_scales.bitcast(I32)
+        for q in range(QUADRANTS):
+            nc.gpsimd.dma_start(
+                wa_plane[32 * q : 32 * q + 4, :, :].bitcast(I32),
+                wa_rows[:, 4 * q : 4 * q + 4, :].rearrange("z r c -> r z c"),
+            )
+
+        wb_raw = [sb.tile([P, PACK, N], F32, name="wb_raw%d" % z) for z in range(PASSES)]
+        xt_table = [sb.tile([P, T], U32, name="xt_table%d" % z) for z in range(PASSES)]
+        wa_codes = [sb.tile([P, N], U32, name="wa_codes%d" % z, align_bytes=64) for z in range(PASSES)]
+        tb_rows = [sb.tile([P, C], F32, name="tb_rows%d" % i) for i in range(J_TILES)]
+        bias_col = sb.tile([P, 2], F32, name="bias_col")
+
+        def load_words(dst, words, z):
+            nc.sync.dma_start(dst[:].bitcast(I32), words[z].rearrange("p c r -> p (c r)").bitcast(I32))
+
+        for z in range(PASSES):
+            rows = wb[z * K_PASS : (z + 1) * K_PASS, :]
+            nc.sync.dma_start(wb_raw[z][:], rows.rearrange("(p r) n -> p r n", r=PACK))
+        nc.sync.dma_start(entries[:], offs2)
+        nc.scalar.dma_start(bias_col[:], bi.rearrange("o (p e) -> p (o e)", e=2))
+        for z in range(PASSES):
+            load_words(xt_table[z], xt_words, z)
+            load_words(wa_codes[z], wa_words, z)
+        for i in range(J_TILES):
+            nc.sync.dma_start(tb_rows[i][:], tb[i * P : (i + 1) * P, :])
+
+        ident = sb.tile([P, P], F32, name="ident")
+        make_identity(nc, ident[:])
+        bias_ps = ps.tile([P, 2, P], F32, name="bias_ps")
+        for e in range(2):
+            nc.tensor.transpose(bias_ps[:, e, :], bias_col[:, e : e + 1].to_broadcast([P, P]), ident[:])
+        bias = sb.tile([P, N], F32, name="bias")
+        nc.scalar.activation(
+            bias[:].rearrange("p (q e) -> p q e", e=2), bias_ps[:].rearrange("p e q -> p q e"), COPY
+        )
+
+        wb_codes = [sb.tile([P, N], U32, name="wb_codes%d" % z, align_bytes=64) for z in range(PASSES)]
+        wb_plane = [sb.tile([P, N], U8, name="wb_plane%d" % z, align_bytes=64) for z in range(PASSES)]
+        wb_grouped = [sb.tile([P, N, PACK], BF16, name="wb_grouped%d" % z, align_bytes=64) for z in range(PASSES)]
+        x_plane = sb.tile([P, PASSES, J], U8, name="x_plane", align_bytes=64)
+
+        def weave(z):
+            dst = wb_grouped[z][:].rearrange("p (c i) r -> p c r i", i=4)
+            src = wb_raw[z][:].rearrange("p r (c i) -> p c r i", i=4)
+            return dst, src
+
+        def quantise(z):
+            nc.vector.quantize_mx(
+                out=wb_codes[z][:].bitcast(E5M2),
+                scales=wb_plane[z][:],
+                in_=wb_grouped[z][:].rearrange("p n r -> p (n r)"),
+            )
+
+        nc.vector.tensor_copy(*weave(0))
+        nc.scalar.copy(*weave(1))
+        nc.vector.tensor_copy(x_plane[:, 0, :], xt_plane[:, 0, :].indirect(tokens[:]))
+        quantise(0)
+        nc.vector.tensor_copy(x_plane[:, 1, :], xt_plane[:, 1, :].indirect(tokens[:]))
+
+        x_codes = [
+            [sb.tile([P, P], U32, name="x_codes%d_%d" % (z, i), align_bytes=64) for i in range(J_TILES)]
+            for z in range(PASSES)
+        ]
+        a_ps = [ps.tile([P, N], F32, name="a_ps%d" % i) for i in range(J_TILES)]
+        b_ps = [ps.tile([P, N], F32, name="b_ps%d" % i) for i in range(J_TILES)]
+
+        def gather_words(z):
+            for i in range(J_TILES):
+                part = tokens[:, i * (P // 16) : (i + 1) * (P // 16)]
+                nc.vector.tensor_copy(x_codes[z][i][:], xt_table[z][:].indirect(part))
+
+        def product(acc, z, i, codes, plane):
+            nc.tensor.matmul_mx(
+                out=acc[:],
+                lhsT=x_codes[z][i][:].bitcast(E4M3),
+                lhsT_scale=x_plane[:, z, i * P : (i + 1) * P],
+                rhs=codes.bitcast(E5M2),
+                rhs_scale=plane,
+                start=(z == 0),
+                stop=(z == PASSES - 1),
+            )
+
+        gather_words(0)
+        quantise(1)
+        gather_words(1)
+        for z in range(PASSES):
+            for i in range(J_TILES):
+                product(b_ps[i], z, i, wb_codes[z][:], wb_plane[z][:])
+            for i in range(J_TILES):
+                product(a_ps[i], z, i, wa_codes[z][:], wa_plane[:, z, :])
+
+        gate = [sb.tile([P, N], F32, name="gate%d" % i) for i in range(J_TILES)]
+        biased = [sb.tile([P, N], F32, name="biased%d" % i) for i in range(J_TILES)]
+        mixed = [sb.tile([P, N], F32, name="mixed%d" % i) for i in range(J_TILES)]
+        result = [sb.tile([P, N], F32, name="result%d" % i) for i in range(J_TILES)]
+        for i in range(J_TILES):
+            nc.scalar.activation(gate[i][:], tb_rows[i][:].indirect(entries[:]), COPY)
+        for i in range(J_TILES):
+            nc.vector.tensor_tensor(biased[i][:], b_ps[i][:], bias[:], ADD)
+        for i in range(J_TILES):
+            nc.vector.scalar_tensor_tensor(mixed[i][:], biased[i][:], 0.5, a_ps[i][:], MULT, ADD)
+        for i in range(J_TILES):
+            nc.vector.tensor_tensor(result[i][:], mixed[i][:], gate[i][:], MULT)
+            nc.sync.dma_start(out[i * P : (i + 1) * P, :], result[i][:])

@@ -1,7 +1,6 @@
 from contextlib import ExitStack
 
 import concourse.mybir as mybir
-from concourse.masks import make_identity
 
 K, T, J, N, C = 1024, 1024, 256, 256, 512
 FLOPS = 2 * 2 * K * J * N
@@ -44,51 +43,55 @@ def tile_list_rows_onetoken_tablegate_kernel(
         nc.vector.memset(xt_plane[:].rearrange("p z c -> p (z c)").bitcast(I32), 0)
         nc.vector.memset(wa_plane[:].rearrange("p z c -> p (z c)").bitcast(I32), 0)
 
-        nc.sync.dma_start(tokens[:], offs)
-        xt_rows = xt_scales.bitcast(I32)
-        for q in range(QUADRANTS):
-            nc.scalar.dma_start(
-                xt_plane[32 * q : 32 * q + 4, :, :].bitcast(I32),
-                xt_rows[:, 4 * q : 4 * q + 4, :].rearrange("z r c -> r z c"),
-            )
-        wa_rows = wa_scales.bitcast(I32)
-        for q in range(QUADRANTS):
-            nc.gpsimd.dma_start(
-                wa_plane[32 * q : 32 * q + 4, :, :].bitcast(I32),
-                wa_rows[:, 4 * q : 4 * q + 4, :].rearrange("z r c -> r z c"),
-            )
-
         wb_raw = [sb.tile([P, PACK, N], F32, name="wb_raw%d" % z) for z in range(PASSES)]
-        xt_table = [sb.tile([P, T], U32, name="xt_table%d" % z) for z in range(PASSES)]
+        xt_table = [sb.tile([P, T], U32, name="xt_table%d" % z, tag="xt_table%d" % z, align_bytes=64) for z in range(PASSES)]
         wa_codes = [sb.tile([P, N], U32, name="wa_codes%d" % z, align_bytes=64) for z in range(PASSES)]
-        tb_rows = [sb.tile([P, C], F32, name="tb_rows%d" % i) for i in range(J_TILES)]
-        bias_col = sb.tile([P, 2], F32, name="bias_col")
+        bias_col = sb.tile([P, 8], F32, name="bias_col")
 
-        def load_words(dst, words, z):
-            nc.sync.dma_start(dst[:].bitcast(I32), words[z].rearrange("p c r -> p (c r)").bitcast(I32))
-
-        for z in range(PASSES):
+        def load_wb(z):
             rows = wb[z * K_PASS : (z + 1) * K_PASS, :]
             nc.sync.dma_start(wb_raw[z][:], rows.rearrange("(p r) n -> p r n", r=PACK))
+
+        def load_xt(z):
+            nc.sync.dma_start(xt_table[z][:].bitcast(I32), xt_words[z].rearrange("p c r -> p (c r)").bitcast(I32))
+
+        def load_wa(z):
+            nc.sync.dma_start(wa_codes[z][:].bitcast(I32), wa_words[z].rearrange("p c r -> p (c r)").bitcast(I32))
+
+        def load_scales(queue, plane, scales, q):
+            queue.dma_start(
+                plane[q:P:32, :, :].bitcast(I32),
+                scales.bitcast(I32)[:, q:16:4, :].rearrange("z r c -> r z c"),
+            )
+
+        tb_rows = [sb.tile([P, C], F32, name="tb_rows%d" % i) for i in range(J_TILES)]
+        nc.sync.dma_start(tokens[:], offs)
+        nc.scalar.dma_start(bias_col[:], bi.rearrange("o (j b) -> o j b", b=8).to_broadcast([4, 32, 8]))
+        load_wb(0)
+        for q in range(QUADRANTS):
+            load_scales(nc.sync, xt_plane, xt_scales, q)
+        load_wb(1)
+        load_xt(0)
+        for q in range(QUADRANTS):
+            load_scales(nc.sync, wa_plane, wa_scales, q)
+        load_wa(0)
+        load_xt(1)
+        load_wa(1)
+        nc.sync.dma_start(tb_rows[0][:], tb[0:P, :])
         nc.sync.dma_start(entries[:], offs2)
-        nc.scalar.dma_start(bias_col[:], bi.rearrange("o (p e) -> p (o e)", e=2))
-        for z in range(PASSES):
-            load_words(xt_table[z], xt_words, z)
-            load_words(wa_codes[z], wa_words, z)
-        for i in range(J_TILES):
-            nc.sync.dma_start(tb_rows[i][:], tb[i * P : (i + 1) * P, :])
+        nc.sync.dma_start(tb_rows[1][:], tb[P : 2 * P, :])
 
-        ident = sb.tile([P, P], F32, name="ident")
-        make_identity(nc, ident[:])
-        bias_ps = ps.tile([P, 2, P], F32, name="bias_ps")
-        for e in range(2):
-            nc.tensor.transpose(bias_ps[:, e, :], bias_col[:, e : e + 1].to_broadcast([P, P]), ident[:])
+        spread = sb.tile([P, 8, 32], F32, name="spread", align_bytes=64)
+        turned = sb.tile([P, 8, 32], F32, name="turned", align_bytes=64)
         bias = sb.tile([P, N], F32, name="bias")
-        nc.scalar.activation(
-            bias[:].rearrange("p (q e) -> p q e", e=2), bias_ps[:].rearrange("p e q -> p q e"), COPY
-        )
+        nc.vector.tensor_copy(spread[:], bias_col[:].unsqueeze(2).to_broadcast([P, 8, 32]))
+        nc.vector.transpose(turned[:].rearrange("p b j -> p (b j)"), spread[:].rearrange("p b i -> p (b i)"))
+        nc.vector.tensor_copy(bias[:].rearrange("p (j b) -> p j b", b=8), turned[:].rearrange("p b j -> p j b"))
 
-        wb_codes = [sb.tile([P, N], U32, name="wb_codes%d" % z, align_bytes=64) for z in range(PASSES)]
+        wb_codes = [
+            sb.tile([P, N], U32, name="wb_codes0", align_bytes=64),
+            sb.tile([P, N], U32, name="wb_codes1", tag="xt_table0", align_bytes=64),
+        ]
         wb_plane = [sb.tile([P, N], U8, name="wb_plane%d" % z, align_bytes=64) for z in range(PASSES)]
         wb_grouped = [sb.tile([P, N, PACK], BF16, name="wb_grouped%d" % z, align_bytes=64) for z in range(PASSES)]
         x_plane = sb.tile([P, PASSES, J], U8, name="x_plane", align_bytes=64)
@@ -105,11 +108,11 @@ def tile_list_rows_onetoken_tablegate_kernel(
                 in_=wb_grouped[z][:].rearrange("p n r -> p (n r)"),
             )
 
-        nc.vector.tensor_copy(*weave(0))
+        nc.scalar.copy(*weave(0))
         nc.scalar.copy(*weave(1))
         nc.vector.tensor_copy(x_plane[:, 0, :], xt_plane[:, 0, :].indirect(tokens[:]))
-        quantise(0)
         nc.vector.tensor_copy(x_plane[:, 1, :], xt_plane[:, 1, :].indirect(tokens[:]))
+        quantise(0)
 
         x_codes = [
             [sb.tile([P, P], U32, name="x_codes%d_%d" % (z, i), align_bytes=64) for i in range(J_TILES)]

@@ -76,8 +76,8 @@ def tile_list_rows_onetoken_tablegate_kernel(
             load_scales(nc.sync, wa_plane, wa_scales, q)
         load_wa(0)
         load_xt(1)
-        load_wa(1)
         nc.sync.dma_start(tb_rows[0][:], tb[0:P, :])
+        load_wa(1)
         nc.sync.dma_start(entries[:], offs2)
         nc.sync.dma_start(tb_rows[1][:], tb[P : 2 * P, :])
 

from contextlib import ExitStack

import concourse.mybir as mybir

K, T, J, N, C = 1024, 1024, 256, 256, 512
FLOPS = 2 * 2 * K * J * N

F32 = mybir.dt.float32
BF16 = mybir.dt.bfloat16
I32 = mybir.dt.int32
U32 = mybir.dt.uint32
U16 = mybir.dt.uint16
U8 = mybir.dt.uint8
E4M3 = mybir.dt.float8_e4m3fn_x4
E5M2 = mybir.dt.float8_e5m2_x4
ADD = mybir.AluOpType.add
MULT = mybir.AluOpType.mult
COPY = mybir.ActivationFunctionType.Copy

P = 128
PACK = 4
K_PASS = P * PACK
PASSES = K // K_PASS
J_TILES = J // P
LIST_COLS = J // 16
QUADRANTS = 4


def tile_list_rows_onetoken_tablegate_kernel(
    tc, xt_words, xt_scales, wa_words, wa_scales, wb, bi, tb, offs, offs2, out
):
    nc = tc.nc
    with ExitStack() as ctx:
        lists = ctx.enter_context(tc.tile_pool(name="lists", bufs=1))
        sb = ctx.enter_context(tc.tile_pool(name="sb", bufs=1))
        ps = ctx.enter_context(tc.psum_pool(name="ps", bufs=1))

        tokens = lists.tile([P, LIST_COLS], U16, name="tokens")
        entries = lists.tile([P, N // 16], U16, name="entries")

        xt_plane = sb.tile([P, PASSES, T], U8, name="xt_plane", align_bytes=64)
        wa_plane = sb.tile([P, PASSES, N], U8, name="wa_plane", align_bytes=64)
        nc.vector.memset(xt_plane[:].rearrange("p z c -> p (z c)").bitcast(I32), 0)
        nc.vector.memset(wa_plane[:].rearrange("p z c -> p (z c)").bitcast(I32), 0)

        wb_raw = [sb.tile([P, PACK, N], F32, name="wb_raw%d" % z) for z in range(PASSES)]
        xt_table = [sb.tile([P, T], U32, name="xt_table%d" % z, tag="xt_table%d" % z, align_bytes=64) for z in range(PASSES)]
        wa_codes = [sb.tile([P, N], U32, name="wa_codes%d" % z, align_bytes=64) for z in range(PASSES)]
        bias_col = sb.tile([P, 8], F32, name="bias_col")

        def load_wb(z):
            rows = wb[z * K_PASS : (z + 1) * K_PASS, :]
            nc.sync.dma_start(wb_raw[z][:], rows.rearrange("(p r) n -> p r n", r=PACK))

        def load_xt(z):
            nc.sync.dma_start(xt_table[z][:].bitcast(I32), xt_words[z].rearrange("p c r -> p (c r)").bitcast(I32))

        def load_wa(z):
            nc.sync.dma_start(wa_codes[z][:].bitcast(I32), wa_words[z].rearrange("p c r -> p (c r)").bitcast(I32))

        def load_scales(queue, plane, scales, q):
            queue.dma_start(
                plane[q:P:32, :, :].bitcast(I32),
                scales.bitcast(I32)[:, q:16:4, :].rearrange("z r c -> r z c"),
            )

        tb_rows = [sb.tile([P, C], F32, name="tb_rows%d" % i) for i in range(J_TILES)]
        nc.sync.dma_start(tokens[:], offs)
        nc.scalar.dma_start(bias_col[:], bi.rearrange("o (j b) -> o j b", b=8).to_broadcast([4, 32, 8]))
        load_wb(0)
        for q in range(QUADRANTS):
            load_scales(nc.sync, xt_plane, xt_scales, q)
        load_wb(1)
        load_xt(0)
        for q in range(QUADRANTS):
            load_scales(nc.sync, wa_plane, wa_scales, q)
        load_wa(0)
        load_xt(1)
        nc.sync.dma_start(tb_rows[0][:], tb[0:P, :])
        load_wa(1)
        nc.sync.dma_start(entries[:], offs2)
        nc.sync.dma_start(tb_rows[1][:], tb[P : 2 * P, :])

        spread = sb.tile([P, 8, 32], F32, name="spread", align_bytes=64)
        turned = sb.tile([P, 8, 32], F32, name="turned", align_bytes=64)
        bias = sb.tile([P, N], F32, name="bias")
        nc.vector.tensor_copy(spread[:], bias_col[:].unsqueeze(2).to_broadcast([P, 8, 32]))
        nc.vector.transpose(turned[:].rearrange("p b j -> p (b j)"), spread[:].rearrange("p b i -> p (b i)"))
        nc.vector.tensor_copy(bias[:].rearrange("p (j b) -> p j b", b=8), turned[:].rearrange("p b j -> p j b"))

        wb_codes = [
            sb.tile([P, N], U32, name="wb_codes0", align_bytes=64),
            sb.tile([P, N], U32, name="wb_codes1", tag="xt_table0", align_bytes=64),
        ]
        wb_plane = [sb.tile([P, N], U8, name="wb_plane%d" % z, align_bytes=64) for z in range(PASSES)]
        wb_grouped = [sb.tile([P, N, PACK], BF16, name="wb_grouped%d" % z, align_bytes=64) for z in range(PASSES)]
        x_plane = sb.tile([P, PASSES, J], U8, name="x_plane", align_bytes=64)

        def weave(z):
            dst = wb_grouped[z][:].rearrange("p (c i) r -> p c r i", i=4)
            src = wb_raw[z][:].rearrange("p r (c i) -> p c r i", i=4)
            return dst, src

        def quantise(z):
            nc.vector.quantize_mx(
                out=wb_codes[z][:].bitcast(E5M2),
                scales=wb_plane[z][:],
                in_=wb_grouped[z][:].rearrange("p n r -> p (n r)"),
            )

        nc.scalar.copy(*weave(0))
        nc.scalar.copy(*weave(1))
        nc.vector.tensor_copy(x_plane[:, 0, :], xt_plane[:, 0, :].indirect(tokens[:]))
        nc.vector.tensor_copy(x_plane[:, 1, :], xt_plane[:, 1, :].indirect(tokens[:]))
        quantise(0)

        x_codes = [
            [sb.tile([P, P], U32, name="x_codes%d_%d" % (z, i), align_bytes=64) for i in range(J_TILES)]
            for z in range(PASSES)
        ]
        a_ps = [ps.tile([P, N], F32, name="a_ps%d" % i) for i in range(J_TILES)]
        b_ps = [ps.tile([P, N], F32, name="b_ps%d" % i) for i in range(J_TILES)]

        def gather_words(z):
            for i in range(J_TILES):
                part = tokens[:, i * (P // 16) : (i + 1) * (P // 16)]
                nc.vector.tensor_copy(x_codes[z][i][:], xt_table[z][:].indirect(part))

        def product(acc, z, i, codes, plane):
            nc.tensor.matmul_mx(
                out=acc[:],
                lhsT=x_codes[z][i][:].bitcast(E4M3),
                lhsT_scale=x_plane[:, z, i * P : (i + 1) * P],
                rhs=codes.bitcast(E5M2),
                rhs_scale=plane,
                start=(z == 0),
                stop=(z == PASSES - 1),
            )

        gather_words(0)
        quantise(1)
        gather_words(1)
        for z in range(PASSES):
            for i in range(J_TILES):
                product(b_ps[i], z, i, wb_codes[z][:], wb_plane[z][:])
            for i in range(J_TILES):
                product(a_ps[i], z, i, wa_codes[z][:], wa_plane[:, z, :])

        gate = [sb.tile([P, N], F32, name="gate%d" % i) for i in range(J_TILES)]
        biased = [sb.tile([P, N], F32, name="biased%d" % i) for i in range(J_TILES)]
        mixed = [sb.tile([P, N], F32, name="mixed%d" % i) for i in range(J_TILES)]
        result = [sb.tile([P, N], F32, name="result%d" % i) for i in range(J_TILES)]
        for i in range(J_TILES):
            nc.scalar.activation(gate[i][:], tb_rows[i][:].indirect(entries[:]), COPY)
        for i in range(J_TILES):
            nc.vector.tensor_tensor(biased[i][:], b_ps[i][:], bias[:], ADD)
        for i in range(J_TILES):
            nc.vector.scalar_tensor_tensor(mixed[i][:], biased[i][:], 0.5, a_ps[i][:], MULT, ADD)
        for i in range(J_TILES):
            nc.vector.tensor_tensor(result[i][:], mixed[i][:], gate[i][:], MULT)
            nc.sync.dma_start(out[i * P : (i + 1) * P, :], result[i][:])
